import numpy as np
import ml_dtypes


def mxq(x, axis, fmt="e4m3"):
    dtype, down = {"e4m3": (ml_dtypes.float8_e4m3fn, 7), "e5m2": (ml_dtypes.float8_e5m2, 14)}[fmt]
    v = np.moveaxis(np.asarray(x, np.float32).astype(ml_dtypes.bfloat16).astype(np.float64), axis, -1)
    blocks = v.reshape(v.shape[:-1] + (-1, 32))
    amax = np.abs(blocks).max(-1, keepdims=True)
    byte = np.maximum(np.where(amax > 0, np.frexp(amax)[1] - 1 + 127, 0) - down, 1)
    scale = np.exp2(byte - 127.0)
    codes = (blocks / scale).astype(np.float32).astype(dtype).astype(np.float64)
    return np.moveaxis((codes * scale).reshape(v.shape), -1, axis)


WIDE = False


def mx_kscale(k):
    if not WIDE:
        return np.ones(k)
    levels = np.array([10, -10, 5, -5, 0])
    if k % 512:
        return np.exp2(np.random.permutation(np.resize(levels, k // 32))).repeat(32)
    a = np.empty((k // 512, 16))
    for p in range(k // 512):
        a[p, :8] = np.random.permutation(np.resize(levels, 8))
        for g in range(8):
            far = levels[np.abs(levels - a[p, g]) >= 10]
            a[p, g + 8] = far[np.random.randint(len(far))]
    return np.exp2(a.ravel()).repeat(32)


def f64(x):
    return np.asarray(x).astype(np.float64)


def striped(idx):
    return np.tile(idx.reshape(-1, 16).T, (8, 1)).astype(np.uint16)


def unstriped(offs):
    return offs[:16].T.reshape(-1).astype(np.int64)


E2M1 = np.array([0.0, 0.5, 1.0, 1.5, 2.0, 3.0, 4.0, 6.0, -0.0, -0.5, -1.0, -1.5, -2.0, -3.0, -4.0, -6.0])


def pack_weight(w, fmt):
    k, n = w.shape
    w = f64(np.asarray(w, np.float32).astype(ml_dtypes.bfloat16)).reshape(k // 32, 32, n)
    amax = np.abs(w).max(1)
    if fmt == "e4m3":
        byte = np.frexp(amax)[1] - 1 + 127 - 7
    else:
        mant, ex = np.frexp(amax / 6.0)
        byte = np.where(mant > 0.5, ex, ex - 1) + 127
    byte = np.clip(np.where(amax > 0, byte, 1), 1, 254)
    scaled = (w * np.exp2(127.0 - byte)[:, None, :]).reshape(k, n).astype(np.float32)
    by_word = np.ascontiguousarray(scaled.reshape(k // 512, 128, 4, n).transpose(0, 1, 3, 2))
    if fmt == "e4m3":
        words = by_word.astype(ml_dtypes.float8_e4m3fn).view(np.uint8)
    else:
        c = by_word.astype(ml_dtypes.float4_e2m1fn).view(np.uint8) & 0xF
        words = (c[..., 0::2] | (c[..., 1::2] << 4)).reshape(k // 512, 128, 2 * n)
    return np.ascontiguousarray(words), np.ascontiguousarray(byte.astype(np.uint8).reshape(k // 512, 16, n))


def unpack_weight(words, scales, fmt):
    g, _, n = scales.shape
    words = np.ascontiguousarray(words).reshape(g, 128, n, -1)
    if fmt == "e4m3":
        vals = words.view(ml_dtypes.float8_e4m3fn).astype(np.float64)
    else:
        nib = np.empty((g, 128, n, 4), np.uint8)
        nib[..., 0::2] = words & 0xF
        nib[..., 1::2] = words >> 4
        vals = E2M1[nib]
    vals = vals * np.repeat(np.exp2(scales.astype(np.float64) - 127.0), 8, axis=1)[..., None]
    return vals.transpose(0, 1, 3, 2).reshape(g * 512, n)


def gelu(v):
    return 0.5 * v * (1.0 + np.tanh(np.sqrt(2.0 / np.pi) * (v + 0.044715 * v**3)))


K, T, S, H, T2, N, P = 1024, 2048, 1024, 1024, 2048, 512, 128

def setup_inputs():
    n = np.random.standard_normal
    s = mx_kscale(K)[:, None]
    u = mx_kscale(H)[:, None]
    tab_words, tab_scales = pack_weight(n((K, T)) * s, "e4m3")
    w4_words, w4_scales = pack_weight(n((H, N)) / np.sqrt(H) / u, "e2m1")
    return {
        "tab_words": tab_words, "tab_scales": tab_scales,
        "offs": striped(np.random.permutation(T)[:S]),
        "w1": (n((K, H)) / np.sqrt(K) / s).astype(np.float32),
        "b": (0.5 * n(H)).astype(np.float32),
        "offs2": striped(np.random.permutation(T2)[:S]),
        "wgs": np.exp(0.3 * n((P, S))).astype(np.float32),
        "old": (n((H, T2)) * u).astype(np.float32),
        "w4_words": w4_words, "w4_scales": w4_scales,
    }

def reference(tab_words, tab_scales, offs, w1, b, offs2, wgs, old, w4_words, w4_scales):
    v = unpack_weight(tab_words, tab_scales, "e4m3")[:, unstriped(offs)]
    w1q = mxq(f64(w1), 0, "e4m3")
    h = (w1q.T @ v) + f64(b)[:, None]
    page = np.zeros((H, T2))
    page[:, unstriped(offs2)] = np.tile(f64(wgs), (H // P, 1)) * h
    gate = 1.0 / (1.0 + np.exp(-page))
    z = f64(old) * gate
    zq = mxq(z, 0, "e4m3")
    w4 = unpack_weight(w4_words, w4_scales, "e2m1")
    return w4.T @ zq

@@ -1,0 +1,270 @@
+from contextlib import ExitStack
+
+import concourse.mybir as mybir
+
+K, T, S, H, T2, N = 1024, 2048, 1024, 1024, 2048, 512
+FLOPS = 2 * K * H * S + 2 * H * N * T2
+
+F32 = mybir.dt.float32
+BF16 = mybir.dt.bfloat16
+I32 = mybir.dt.int32
+U32 = mybir.dt.uint32
+U16 = mybir.dt.uint16
+U8 = mybir.dt.uint8
+FP8X4 = mybir.dt.float8_e4m3fn_x4
+FP4X4 = mybir.dt.float4_e2m1fn_x4
+ACT = mybir.ActivationFunctionType
+MULT = mybir.AluOpType.mult
+
+P = 128
+PACK = 4
+KP = P * PACK
+BANK = 512
+QUADS = 4
+QP = 32
+
+
+def tile_list_valve_command_response_kernel(
+    tc, tab_words, tab_scales, offs, w1, b, offs2, wgs, old, w4_words, w4_scales, out
+):
+    nc = tc.nc
+    with ExitStack() as ctx:
+        keep = ctx.enter_context(tc.tile_pool(name="keep", bufs=1))
+        big = ctx.enter_context(tc.tile_pool(name="big", bufs=8))
+        ring = ctx.enter_context(tc.tile_pool(name="ring", bufs=3))
+        psum = ctx.enter_context(tc.psum_pool(name="psum", bufs=8))
+
+        idx = keep.tile([P, S // 16], U16, name="idx")
+        idx2 = keep.tile([P, S // 16], U16, name="idx2")
+        tab_s = keep.tile([P, T], U8, name="tab_s", align_bytes=64)
+        tab_w = [keep.tile([P, T], U32, name="tab_w%d" % a, align_bytes=64) for a in range(2)]
+        v_s = keep.tile([P, S], U8, name="v_s", align_bytes=64)
+        v_w = [keep.tile([P, S], U32, name="v_w%d" % a, align_bytes=64) for a in range(2)]
+        pages = [keep.tile([P, T2], F32, name="page%d" % i, align_bytes=64) for i in range(2)]
+        bias = keep.tile([P, 2, PACK], F32, name="bias")
+        wg_first = keep.tile([P, S], F32, name="wg_first")
+        wg_rest = keep.tile([P, PACK - 1, S], F32, name="wg_rest")
+        gate = keep.tile([P, PACK, T2], F32, name="gate", align_bytes=64)
+        w1_w = {}
+        w1_s = {}
+        for g in range(2):
+            for a in range(2):
+                w1_w[(a, g)] = keep.tile([P, KP], U32, name="w1_w%d%d" % (a, g), align_bytes=64)
+                w1_s[(a, g)] = keep.tile([P, KP], U8, name="w1_s%d%d" % (a, g), align_bytes=64)
+        z_w = [keep.tile([P, T2], U32, name="z_w%d" % g, align_bytes=64) for g in range(2)]
+        z_s = [keep.tile([P, T2], U8, name="z_s%d" % g, align_bytes=64) for g in range(2)]
+        w4_w = keep.tile([P, 2, 2 * N], U8, name="w4_w", align_bytes=64)
+        w4_s = keep.tile([P, 2 * N], U8, name="w4_s", align_bytes=64)
+
+        nc.vector.memset(tab_s[:].bitcast(U32), 0)
+        for page in pages:
+            nc.vector.memset(page[:], 0.0)
+        nc.vector.memset(w4_s[:].bitcast(U32), 0)
+
+        def load_w1(a, g):
+            raw = big.tile([P, PACK, KP], F32, name="raw", tag="big", align_bytes=64)
+            rows = w1[a * KP : (a + 1) * KP, g * KP : (g + 1) * KP]
+            nc.sync.dma_start(out=raw[:], in_=rows.rearrange("(p i) c -> p i c", i=PACK))
+            return raw
+
+        def load_old(g, c):
+            tile = big.tile([P, PACK, BANK], F32, name="old_sb", tag="big", align_bytes=64)
+            rows = old[g * KP : (g + 1) * KP, c * BANK : (c + 1) * BANK]
+            nc.sync.dma_start(out=tile[:], in_=rows.rearrange("(p t) c -> p t c", t=PACK))
+            return tile
+
+        def load_table_words(a):
+            nc.sync.dma_start(
+                out=tab_w[a][:].bitcast(I32),
+                in_=tab_words[a].rearrange("p t i -> p (t i)").bitcast(I32),
+            )
+
+        nc.sync.dma_start(idx[:], offs)
+        for q in range(QUADS):
+            nc.sync.dma_start(
+                out=tab_s[QP * q : QP * q + 8, :].bitcast(I32),
+                in_=tab_scales[:, 4 * q : 4 * q + 4, :].bitcast(I32),
+            )
+        load_table_words(0)
+        w1_raw = {(0, 0): load_w1(0, 0), (1, 0): load_w1(1, 0)}
+        load_table_words(1)
+        nc.sync.dma_start(idx2[:], offs2)
+        nc.sync.dma_start(out=bias[:], in_=b.rearrange("(g p t) -> p g t", g=2, t=PACK))
+        wgs_dealt = wgs.rearrange("(q t) j -> q t j", t=PACK)
+        for q in range(QUADS):
+            nc.sync.dma_start(out=wg_first[QP * q : QP * (q + 1), :], in_=wgs_dealt[:, 0, :])
+        for q in range(QUADS):
+            nc.sync.dma_start(out=wg_rest[QP * q : QP * (q + 1), :, :], in_=wgs_dealt[:, 1:PACK, :])
+        for a in range(2):
+            w1_raw[(a, 1)] = load_w1(a, 1)
+        old_sb = {(0, c): load_old(0, c) for c in range(4)}
+        nc.sync.dma_start(
+            out=w4_w[:].bitcast(I32), in_=w4_words.rearrange("a p e -> p a e").bitcast(I32)
+        )
+        for q in range(QUADS):
+            nc.sync.dma_start(
+                out=w4_s[QP * q : QP * q + 4, :].rearrange("r (a n) -> r a n", a=2).bitcast(I32),
+                in_=w4_scales[:, 4 * q : 4 * q + 4, :].rearrange("a r n -> r a n").bitcast(I32),
+            )
+        for c in range(4):
+            old_sb[(1, c)] = load_old(1, c)
+
+        def round_w1(a, g, on_vector):
+            grouped = ring.tile([P, PACK, P, PACK], BF16, name="w1_bf", align_bytes=64)
+            dst = grouped[:].rearrange("p t m i -> p m i t")
+            src = w1_raw[(a, g)][:].rearrange("p i (m t) -> p m i t", t=PACK)
+            if on_vector:
+                nc.vector.tensor_copy(out=dst, in_=src)
+            else:
+                nc.scalar.activation(out=dst, in_=src, func=ACT.Copy)
+            return grouped
+
+        def quantize_w1(a, g, grouped):
+            nc.vector.quantize_mx(
+                out=w1_w[(a, g)][:].bitcast(FP8X4),
+                scales=w1_s[(a, g)][:],
+                in_=grouped[:].rearrange("p t m i -> p (t m i)"),
+            )
+
+        def gather_words(a, lo, hi):
+            nc.vector.tensor_copy(
+                out=v_w[a][:, lo:hi], in_=tab_w[a][:].indirect(idx[:, lo // 16 : hi // 16])
+            )
+
+        def signals(g, t):
+            h = ring.tile([P, S], F32, name="h", align_bytes=64)
+            m = slice(t * P, (t + 1) * P)
+            for half in range(2):
+                cols = slice(half * BANK, (half + 1) * BANK)
+                acc = psum.tile([P, BANK], F32, name="acc", tag="acc")
+                for a in range(2):
+                    nc.tensor.matmul_mx(
+                        out=acc[:],
+                        lhsT=w1_w[(a, g)][:, m].bitcast(FP8X4),
+                        lhsT_scale=w1_s[(a, g)][:, m],
+                        rhs=v_w[a][:, cols].bitcast(FP8X4),
+                        rhs_scale=v_s[4 * a : P, cols],
+                        start=(a == 0),
+                        stop=(a == 1),
+                    )
+                nc.scalar.activation(
+                    out=h[:, cols], in_=acc[:], func=ACT.Identity, bias=bias[:, g, t : t + 1]
+                )
+            return h
+
+        def place(h, t, lo, hi):
+            wg = wg_first[:, lo:hi] if t == 0 else wg_rest[:, t - 1, lo:hi]
+            nc.vector.tensor_tensor(
+                pages[t % 2][:].indirect(idx2[:, lo // 16 : hi // 16]), h[:, lo:hi], wg, MULT
+            )
+
+        def sigmoid(t, lo, hi):
+            nc.scalar.activation(
+                out=gate[:, t, lo:hi], in_=pages[t % 2][:, lo:hi], func=ACT.Sigmoid
+            )
+
+        def commands(g, c):
+            z_bf = ring.tile([P, BANK * PACK], BF16, name="z_bf", align_bytes=64)
+            nc.vector.tensor_tensor(
+                z_bf[:].rearrange("p (c i t) -> p c t i", i=4, t=PACK),
+                old_sb[(g, c)][:].rearrange("p t (c i) -> p c t i", i=4),
+                gate[:, :, c * BANK : (c + 1) * BANK].rearrange("p t (c i) -> p c t i", i=4),
+                MULT,
+            )
+            return z_bf
+
+        def quantize_z(g, c, z_bf):
+            cols = slice(c * BANK, (c + 1) * BANK)
+            nc.vector.quantize_mx(
+                out=z_w[g][:, cols].bitcast(FP8X4), scales=z_s[g][:, cols], in_=z_bf[:]
+            )
+
+        def response_pass(acc, g, nt, c):
+            cols = slice(c * BANK, (c + 1) * BANK)
+            nc.tensor.matmul_mx(
+                out=acc[:],
+                lhsT=w4_w[:, g, 2 * P * nt : 2 * P * (nt + 1)].bitcast(FP4X4),
+                lhsT_scale=w4_s[:, g * N + P * nt : g * N + P * (nt + 1)],
+                rhs=z_w[g][:, cols].bitcast(FP8X4),
+                rhs_scale=z_s[g][:, cols],
+                start=(g == 0),
+                stop=(g == 1),
+            )
+
+        nc.vector.tensor_copy(out=v_s[:], in_=tab_s[:].indirect(idx[:]))
+        gather_words(0, 0, S)
+        bf00 = round_w1(0, 0, False)
+        bf10 = round_w1(1, 0, True)
+        quantize_w1(0, 0, bf00)
+        quantize_w1(1, 0, bf10)
+        gather_words(1, 0, BANK)
+        gather_words(1, BANK, S)
+
+        hs = {(0, t): signals(0, t) for t in range(2)}
+        place(hs[(0, 0)], 0, 0, BANK)
+        place(hs[(0, 0)], 0, BANK, S)
+        hs[(0, 2)] = signals(0, 2)
+        bf1 = [round_w1(a, 1, False) for a in range(2)]
+        sigmoid(0, 0, T2)
+        place(hs[(0, 1)], 1, 0, S)
+        hs[(0, 3)] = signals(0, 3)
+        for a in range(2):
+            quantize_w1(a, 1, bf1[a])
+        sigmoid(1, 0, T2)
+        place(hs[(0, 2)], 2, 0, S)
+        hs[(1, 0)] = signals(1, 0)
+        sigmoid(2, 0, T2)
+        place(hs[(0, 3)], 3, 0, S)
+        hs[(1, 1)] = signals(1, 1)
+        sigmoid(3, 0, T2)
+        place(hs[(1, 0)], 0, 0, S)
+        hs[(1, 2)] = signals(1, 2)
+        z_bf = [commands(0, 0)]
+        for c in range(1, 4):
+            z_bf.append(commands(0, c))
+            quantize_z(0, c - 1, z_bf[c - 1])
+        sigmoid(0, 0, T2)
+        place(hs[(1, 1)], 1, 0, S)
+        quantize_z(0, 3, z_bf[3])
+        hs[(1, 3)] = signals(1, 3)
+        sigmoid(1, 0, T2)
+        place(hs[(1, 2)], 2, 0, S)
+        accs = {}
+
+        def open_chunk(c):
+            for nt in range(4):
+                accs[(nt, c)] = psum.tile([P, BANK], F32, name="acc", tag="acc")
+                response_pass(accs[(nt, c)], 0, nt, c)
+
+        open_chunk(0)
+        open_chunk(1)
+        sigmoid(2, 0, T2)
+        place(hs[(1, 3)], 3, 0, S)
+        for c in range(4):
+            sigmoid(3, c * BANK, (c + 1) * BANK)
+
+        out_v = out.rearrange("(n p) c -> p n c", p=P)
+
+        def finish_chunk(c):
+            res = big.tile([P, 4, BANK], F32, name="res", tag="big", align_bytes=64)
+            for nt in range(4):
+                response_pass(accs[(nt, c)], 1, nt, c)
+            for nt in range(4):
+                if c == 3 and nt % 2 == 1:
+                    nc.vector.tensor_copy(out=res[:, nt, :], in_=accs[(nt, c)][:])
+                else:
+                    nc.scalar.copy(out=res[:, nt, :], in_=accs[(nt, c)][:])
+                if nt % 2 == 1:
+                    nc.sync.dma_start(
+                        out=out_v[:, nt - 1 : nt + 1, c * BANK : (c + 1) * BANK],
+                        in_=res[:, nt - 1 : nt + 1, :],
+                    )
+            if c + 2 < 4:
+                open_chunk(c + 2)
+
+        z_bf = [commands(1, 0)]
+        for c in range(4):
+            if c + 1 < 4:
+                z_bf.append(commands(1, c + 1))
+            quantize_z(1, c, z_bf[c])
+            finish_chunk(c)

@@ -15,6 +15,7 @@ FP8X4 = mybir.dt.float8_e4m3fn_x4
 FP4X4 = mybir.dt.float4_e2m1fn_x4
 ACT = mybir.ActivationFunctionType
 MULT = mybir.AluOpType.mult
+ADD = mybir.AluOpType.add
 
 P = 128
 PACK = 4
@@ -30,74 +31,166 @@ def tile_list_valve_command_response_kernel(
     nc = tc.nc
     with ExitStack() as ctx:
         keep = ctx.enter_context(tc.tile_pool(name="keep", bufs=1))
-        big = ctx.enter_context(tc.tile_pool(name="big", bufs=8))
-        ring = ctx.enter_context(tc.tile_pool(name="ring", bufs=3))
+        slots = ctx.enter_context(tc.tile_pool(name="slots", bufs=1))
+        eight = ctx.enter_context(tc.tile_pool(name="eight", bufs=8))
         psum = ctx.enter_context(tc.psum_pool(name="psum", bufs=8))
+
+        def slot(n, shape, dtype, name):
+            return slots.tile(shape, dtype, name=name, tag="slot%d" % n, align_bytes=64)
 
         idx = keep.tile([P, S // 16], U16, name="idx")
         idx2 = keep.tile([P, S // 16], U16, name="idx2")
         tab_s = keep.tile([P, T], U8, name="tab_s", align_bytes=64)
-        tab_w = [keep.tile([P, T], U32, name="tab_w%d" % a, align_bytes=64) for a in range(2)]
         v_s = keep.tile([P, S], U8, name="v_s", align_bytes=64)
         v_w = [keep.tile([P, S], U32, name="v_w%d" % a, align_bytes=64) for a in range(2)]
         pages = [keep.tile([P, T2], F32, name="page%d" % i, align_bytes=64) for i in range(2)]
         bias = keep.tile([P, 2, PACK], F32, name="bias")
-        wg_first = keep.tile([P, S], F32, name="wg_first")
-        wg_rest = keep.tile([P, PACK - 1, S], F32, name="wg_rest")
-        gate = keep.tile([P, PACK, T2], F32, name="gate", align_bytes=64)
-        w1_w = {}
-        w1_s = {}
-        for g in range(2):
-            for a in range(2):
-                w1_w[(a, g)] = keep.tile([P, KP], U32, name="w1_w%d%d" % (a, g), align_bytes=64)
-                w1_s[(a, g)] = keep.tile([P, KP], U8, name="w1_s%d%d" % (a, g), align_bytes=64)
-        z_w = [keep.tile([P, T2], U32, name="z_w%d" % g, align_bytes=64) for g in range(2)]
+        wg = [keep.tile([P, S], F32, name="wg%d" % t) for t in range(PACK)]
+        w1_w = [keep.tile([P, 2 * KP], U32, name="w1_w%d" % g, align_bytes=64) for g in range(2)]
+        w1_s = [keep.tile([P, 2 * KP], U8, name="w1_s%d" % g, align_bytes=64) for g in range(2)]
+        z_w = {1: keep.tile([P, T2], U32, name="z_w1", align_bytes=64)}
         z_s = [keep.tile([P, T2], U8, name="z_s%d" % g, align_bytes=64) for g in range(2)]
         w4_w = keep.tile([P, 2, 2 * N], U8, name="w4_w", align_bytes=64)
         w4_s = keep.tile([P, 2 * N], U8, name="w4_s", align_bytes=64)
 
-        nc.vector.memset(tab_s[:].bitcast(U32), 0)
+        nc.gpsimd.memset(tab_s[:].bitcast(U32), 0)
         for page in pages:
             nc.vector.memset(page[:], 0.0)
         nc.vector.memset(w4_s[:].bitcast(U32), 0)
+        for q in range(QUADS):
+            nc.gpsimd.dma_start(
+                out=tab_s[QP * q : QP * q + 8, :].bitcast(I32),
+                in_=tab_scales[:, 4 * q : 4 * q + 4, :].bitcast(I32),
+            )
 
         def load_w1(a, g):
-            raw = big.tile([P, PACK, KP], F32, name="raw", tag="big", align_bytes=64)
+            raw = slot((1, 4)[g] + a, [P, PACK, KP], F32, "raw")
             rows = w1[a * KP : (a + 1) * KP, g * KP : (g + 1) * KP]
             nc.sync.dma_start(out=raw[:], in_=rows.rearrange("(p i) c -> p i c", i=PACK))
             return raw
 
-        def load_old(g, c):
-            tile = big.tile([P, PACK, BANK], F32, name="old_sb", tag="big", align_bytes=64)
-            rows = old[g * KP : (g + 1) * KP, c * BANK : (c + 1) * BANK]
-            nc.sync.dma_start(out=tile[:], in_=rows.rearrange("(p t) c -> p t c", t=PACK))
+        old_dealt = old.rearrange("(g p t) c -> g p t c", g=2, t=PACK)
+
+        def load_old_rows(t):
+            tile = slot(t, [P, T2], F32, "old_rows")
+            nc.sync.dma_start(out=tile[:], in_=old_dealt[0, :, t, :])
+            return tile
+
+        def load_old_chunk(c):
+            tile = slot((4, 1, 2, 3)[c], [P, PACK, BANK], F32, "old_chunk")
+            nc.sync.dma_start(out=tile[:], in_=old_dealt[1, :, :, c * BANK : (c + 1) * BANK])
             return tile
 
         def load_table_words(a):
+            tile = slot(3 * a, [P, T], U32, "tab_w")
             nc.sync.dma_start(
-                out=tab_w[a][:].bitcast(I32),
+                out=tile[:].bitcast(I32),
                 in_=tab_words[a].rearrange("p t i -> p (t i)").bitcast(I32),
             )
+            return tile
+
+        wgs_dealt = wgs.rearrange("(q t) j -> q t j", t=PACK)
+
+        def load_wg(t):
+            for q in range(QUADS):
+                nc.sync.dma_start(out=wg[t][QP * q : QP * (q + 1), :], in_=wgs_dealt[:, t, :])
 
         nc.sync.dma_start(idx[:], offs)
-        for q in range(QUADS):
-            nc.sync.dma_start(
-                out=tab_s[QP * q : QP * q + 8, :].bitcast(I32),
-                in_=tab_scales[:, 4 * q : 4 * q + 4, :].bitcast(I32),
-            )
-        load_table_words(0)
+        tab_w = [load_table_words(0)]
         w1_raw = {(0, 0): load_w1(0, 0), (1, 0): load_w1(1, 0)}
-        load_table_words(1)
+        tab_w.append(load_table_words(1))
         nc.sync.dma_start(idx2[:], offs2)
         nc.sync.dma_start(out=bias[:], in_=b.rearrange("(g p t) -> p g t", g=2, t=PACK))
-        wgs_dealt = wgs.rearrange("(q t) j -> q t j", t=PACK)
-        for q in range(QUADS):
-            nc.sync.dma_start(out=wg_first[QP * q : QP * (q + 1), :], in_=wgs_dealt[:, 0, :])
-        for q in range(QUADS):
-            nc.sync.dma_start(out=wg_rest[QP * q : QP * (q + 1), :, :], in_=wgs_dealt[:, 1:PACK, :])
+        load_wg(0)
+        load_wg(1)
         for a in range(2):
             w1_raw[(a, 1)] = load_w1(a, 1)
-        old_sb = {(0, c): load_old(0, c) for c in range(4)}
+        load_wg(2)
+        load_wg(3)
+
+        def round_w1(a, g, grouped, on_vector, lo=0, hi=P):
+            dst = grouped[:, a, :].rearrange("p (t m i) -> p m i t", t=PACK, i=PACK)[:, lo:hi]
+            src = w1_raw[(a, g)][:].rearrange("p i (m t) -> p m i t", t=PACK)[:, lo:hi]
+            if on_vector:
+                nc.vector.tensor_copy(out=dst, in_=src)
+            else:
+                nc.scalar.activation(out=dst, in_=src, func=ACT.Copy)
+
+        def gather_words(a, lo, hi):
+            nc.vector.tensor_copy(
+                out=v_w[a][:, lo:hi], in_=tab_w[a][:].indirect(idx[:, lo // 16 : hi // 16])
+            )
+
+        def first_product(g, t, half):
+            cols = slice(half * BANK, (half + 1) * BANK)
+            acc = psum.tile([P, BANK], F32, name="acc", tag="acc")
+            for a in range(2):
+                m = slice(a * KP + t * P, a * KP + (t + 1) * P)
+                nc.tensor.matmul_mx(
+                    out=acc[:],
+                    lhsT=w1_w[g][:, m].bitcast(FP8X4),
+                    lhsT_scale=w1_s[g][:, m],
+                    rhs=v_w[a][:, cols].bitcast(FP8X4),
+                    rhs_scale=v_s[4 * a : P, cols],
+                    start=(a == 0),
+                    stop=(a == 1),
+                )
+            return acc
+
+        def signals(g, t):
+            h = eight.tile([P, S], F32, name="h", tag="H", align_bytes=64)
+            for half in range(2):
+                acc = first_product(g, t, half)
+                nc.scalar.activation(
+                    out=h[:, half * BANK : (half + 1) * BANK],
+                    in_=acc[:],
+                    func=ACT.Identity,
+                    bias=bias[:, g, t : t + 1],
+                )
+            return h
+
+        def weigh(dst, h, t):
+            nc.gpsimd.tensor_tensor(dst, h[:], wg[t][:], MULT)
+
+        def place(src, t, lo, hi):
+            nc.vector.tensor_copy(pages[t % 2][:].indirect(idx2[:, lo // 16 : hi // 16]), src)
+
+        gather_words(0, 0, S)
+        nc.vector.tensor_copy(out=v_s[:], in_=tab_s[:].indirect(idx[:]))
+        w1_bf = slot(12, [P, 2, KP * PACK], BF16, "w1_bf")
+        round_w1(0, 0, w1_bf, False)
+        round_w1(1, 0, w1_bf, True, 0, P // 2)
+        round_w1(1, 0, w1_bf, False, P // 2, P)
+        for a in range(2):
+            nc.vector.quantize_mx(
+                out=w1_w[0][:, a * KP : (a + 1) * KP].bitcast(FP8X4),
+                scales=w1_s[0][:, a * KP : (a + 1) * KP],
+                in_=w1_bf[:, a, :],
+            )
+        gather_words(1, 0, BANK)
+        gather_words(1, BANK, S)
+
+        h_first = eight.tile([P, S], F32, name="h", tag="H", align_bytes=64)
+        for half in range(2):
+            cols = slice(half * BANK, (half + 1) * BANK)
+            acc = first_product(0, 0, half)
+            nc.vector.scalar_tensor_tensor(
+                out=h_first[:, cols],
+                in0=acc[:],
+                scalar=bias[:, 0, 0:1],
+                in1=wg[0][:, cols],
+                op0=ADD,
+                op1=MULT,
+            )
+            place(h_first[:, cols], 0, half * BANK, (half + 1) * BANK)
+        hs = {(0, t): signals(0, t) for t in range(1, PACK)}
+        for t in range(1, PACK):
+            weigh(hs[(0, t)][:], hs[(0, t)], t)
+
+        w1_bf = slot(13, [P, 2, KP * PACK], BF16, "w1_bf")
+        for a in range(2):
+            round_w1(a, 1, w1_bf, False)
+        old_rows = [load_old_rows(t) for t in range(PACK)]
         nc.sync.dma_start(
             out=w4_w[:].bitcast(I32), in_=w4_words.rearrange("a p e -> p a e").bitcast(I32)
         )
@@ -106,78 +199,93 @@ def tile_list_valve_command_response_kernel(
                 out=w4_s[QP * q : QP * q + 4, :].rearrange("r (a n) -> r a n", a=2).bitcast(I32),
                 in_=w4_scales[:, 4 * q : 4 * q + 4, :].rearrange("a r n -> r a n").bitcast(I32),
             )
-        for c in range(4):
-            old_sb[(1, c)] = load_old(1, c)
 
-        def round_w1(a, g, on_vector):
-            grouped = ring.tile([P, PACK, P, PACK], BF16, name="w1_bf", align_bytes=64)
-            dst = grouped[:].rearrange("p t m i -> p m i t")
-            src = w1_raw[(a, g)][:].rearrange("p i (m t) -> p m i t", t=PACK)
-            if on_vector:
-                nc.vector.tensor_copy(out=dst, in_=src)
-            else:
-                nc.scalar.activation(out=dst, in_=src, func=ACT.Copy)
-            return grouped
+        z_rows = [slot(10 + half, [P, PACK, T2 // 2], BF16, "z_rows") for half in range(2)]
 
-        def quantize_w1(a, g, grouped):
-            nc.vector.quantize_mx(
-                out=w1_w[(a, g)][:].bitcast(FP8X4),
-                scales=w1_s[(a, g)][:],
-                in_=grouped[:].rearrange("p t m i -> p (t m i)"),
-            )
+        def gate_rows(t):
+            gate = slot((5, 13, 6, 7)[t], [P, T2], F32, "gate_rows")
+            nc.scalar.activation(out=gate[:], in_=pages[t % 2][:], func=ACT.Sigmoid)
+            return gate
 
-        def gather_words(a, lo, hi):
-            nc.vector.tensor_copy(
-                out=v_w[a][:, lo:hi], in_=tab_w[a][:].indirect(idx[:, lo // 16 : hi // 16])
-            )
-
-        def signals(g, t):
-            h = ring.tile([P, S], F32, name="h", align_bytes=64)
-            m = slice(t * P, (t + 1) * P)
+        def commands_rows(t, gate):
             for half in range(2):
-                cols = slice(half * BANK, (half + 1) * BANK)
-                acc = psum.tile([P, BANK], F32, name="acc", tag="acc")
-                for a in range(2):
-                    nc.tensor.matmul_mx(
-                        out=acc[:],
-                        lhsT=w1_w[(a, g)][:, m].bitcast(FP8X4),
-                        lhsT_scale=w1_s[(a, g)][:, m],
-                        rhs=v_w[a][:, cols].bitcast(FP8X4),
-                        rhs_scale=v_s[4 * a : P, cols],
-                        start=(a == 0),
-                        stop=(a == 1),
-                    )
-                nc.scalar.activation(
-                    out=h[:, cols], in_=acc[:], func=ACT.Identity, bias=bias[:, g, t : t + 1]
+                cols = slice(half * (T2 // 2), (half + 1) * (T2 // 2))
+                nc.gpsimd.tensor_tensor(
+                    z_rows[half][:, t, :], old_rows[t][:, cols], gate[:, cols], MULT
                 )
-            return h
 
-        def place(h, t, lo, hi):
-            wg = wg_first[:, lo:hi] if t == 0 else wg_rest[:, t - 1, lo:hi]
-            nc.vector.tensor_tensor(
-                pages[t % 2][:].indirect(idx2[:, lo // 16 : hi // 16]), h[:, lo:hi], wg, MULT
+        gate = [gate_rows(0)]
+        place(hs[(0, 1)][:], 1, 0, S)
+        nc.vector.quantize_mx(
+            out=w1_w[1][:].bitcast(FP8X4),
+            scales=w1_s[1][:],
+            in_=w1_bf[:].rearrange("p a e -> p (a e)"),
+        )
+        for t in range(PACK):
+            hs[(1, t)] = signals(1, t)
+        for t in range(2):
+            weigh(hs[(1, t)][:], hs[(1, t)], t)
+        commands_rows(0, gate[0])
+        gate.append(gate_rows(1))
+        place(hs[(0, 2)][:], 2, 0, S)
+        commands_rows(1, gate[1])
+        gate.append(gate_rows(2))
+        place(hs[(0, 3)][:], 3, 0, S)
+        commands_rows(2, gate[2])
+        late = {2: slot(6, [P, S], F32, "late")}
+        weigh(late[2][:], hs[(1, 2)], 2)
+        gate.append(gate_rows(3))
+        place(hs[(1, 0)][:], 0, 0, S)
+        commands_rows(3, gate[3])
+        late[3] = slot(7, [P, S], F32, "late")
+        weigh(late[3][:], hs[(1, 3)], 3)
+        old_chunks = [load_old_chunk(c) for c in range(4)]
+
+        gates = [slot((0, 5, 8, 9)[c], [P, PACK, BANK], F32, "gate_chunk") for c in range(4)]
+
+        def sigmoid(t):
+            for c in range(4):
+                nc.scalar.activation(
+                    out=gates[c][:, t, :],
+                    in_=pages[t % 2][:, c * BANK : (c + 1) * BANK],
+                    func=ACT.Sigmoid,
+                )
+
+        def interleave(half):
+            z_bf = slot(12 + half, [P, T2 // 2 * PACK], BF16, "z_bf0")
+            for part in range(2):
+                dst = z_bf[:, part * BANK * PACK : (part + 1) * BANK * PACK]
+                src = z_rows[half][:, :, part * BANK : (part + 1) * BANK]
+                if half == 0:
+                    nc.gpsimd.tensor_scalar(
+                        dst.rearrange("p (c t) -> p c t", t=PACK),
+                        src.rearrange("p t c -> p c t"),
+                        1.0,
+                        0.0,
+                        MULT,
+                        ADD,
+                    )
+                else:
+                    nc.scalar.copy(
+                        out=dst.rearrange("p (c i t) -> p c t i", i=4, t=PACK),
+                        in_=src.rearrange("p t (c i) -> p c t i", i=4),
+                    )
+            return z_bf
+
+        def quantize_z(g, lo, hi, z_bf):
+            nc.vector.quantize_mx(
+                out=z_w[g][:, lo:hi].bitcast(FP8X4), scales=z_s[g][:, lo:hi], in_=z_bf[:]
             )
 
-        def sigmoid(t, lo, hi):
-            nc.scalar.activation(
-                out=gate[:, t, lo:hi], in_=pages[t % 2][:, lo:hi], func=ACT.Sigmoid
-            )
-
-        def commands(g, c):
-            z_bf = ring.tile([P, BANK * PACK], BF16, name="z_bf", align_bytes=64)
+        def commands(c):
+            z_bf = eight.tile([P, BANK * PACK], BF16, name="z_bf1", tag="H", align_bytes=64)
             nc.vector.tensor_tensor(
-                z_bf[:].rearrange("p (c i t) -> p c t i", i=4, t=PACK),
-                old_sb[(g, c)][:].rearrange("p t (c i) -> p c t i", i=4),
-                gate[:, :, c * BANK : (c + 1) * BANK].rearrange("p t (c i) -> p c t i", i=4),
+                z_bf[:].rearrange("p (c i t) -> p c t i", i=2, t=PACK),
+                old_chunks[c][:].rearrange("p t (c i) -> p c t i", i=2),
+                gates[c][:].rearrange("p t (c i) -> p c t i", i=2),
                 MULT,
             )
             return z_bf
-
-        def quantize_z(g, c, z_bf):
-            cols = slice(c * BANK, (c + 1) * BANK)
-            nc.vector.quantize_mx(
-                out=z_w[g][:, cols].bitcast(FP8X4), scales=z_s[g][:, cols], in_=z_bf[:]
-            )
 
         def response_pass(acc, g, nt, c):
             cols = slice(c * BANK, (c + 1) * BANK)
@@ -191,44 +299,6 @@ def tile_list_valve_command_response_kernel(
                 stop=(g == 1),
             )
 
-        nc.vector.tensor_copy(out=v_s[:], in_=tab_s[:].indirect(idx[:]))
-        gather_words(0, 0, S)
-        bf00 = round_w1(0, 0, False)
-        bf10 = round_w1(1, 0, True)
-        quantize_w1(0, 0, bf00)
-        quantize_w1(1, 0, bf10)
-        gather_words(1, 0, BANK)
-        gather_words(1, BANK, S)
-
-        hs = {(0, t): signals(0, t) for t in range(2)}
-        place(hs[(0, 0)], 0, 0, BANK)
-        place(hs[(0, 0)], 0, BANK, S)
-        hs[(0, 2)] = signals(0, 2)
-        bf1 = [round_w1(a, 1, False) for a in range(2)]
-        sigmoid(0, 0, T2)
-        place(hs[(0, 1)], 1, 0, S)
-        hs[(0, 3)] = signals(0, 3)
-        for a in range(2):
-            quantize_w1(a, 1, bf1[a])
-        sigmoid(1, 0, T2)
-        place(hs[(0, 2)], 2, 0, S)
-        hs[(1, 0)] = signals(1, 0)
-        sigmoid(2, 0, T2)
-        place(hs[(0, 3)], 3, 0, S)
-        hs[(1, 1)] = signals(1, 1)
-        sigmoid(3, 0, T2)
-        place(hs[(1, 0)], 0, 0, S)
-        hs[(1, 2)] = signals(1, 2)
-        z_bf = [commands(0, 0)]
-        for c in range(1, 4):
-            z_bf.append(commands(0, c))
-            quantize_z(0, c - 1, z_bf[c - 1])
-        sigmoid(0, 0, T2)
-        place(hs[(1, 1)], 1, 0, S)
-        quantize_z(0, 3, z_bf[3])
-        hs[(1, 3)] = signals(1, 3)
-        sigmoid(1, 0, T2)
-        place(hs[(1, 2)], 2, 0, S)
         accs = {}
 
         def open_chunk(c):
@@ -236,17 +306,24 @@ def tile_list_valve_command_response_kernel(
                 accs[(nt, c)] = psum.tile([P, BANK], F32, name="acc", tag="acc")
                 response_pass(accs[(nt, c)], 0, nt, c)
 
+        sigmoid(0)
+        place(hs[(1, 1)][:], 1, 0, S)
+        sigmoid(1)
+        place(late[2][:], 2, 0, S)
+        z_left = interleave(0)
+        z_right = interleave(1)
+        sigmoid(2)
+        place(late[3][:], 3, 0, S)
+        sigmoid(3)
+        z_w[0] = slot(7, [P, T2], U32, "z_w0")
+        quantize_z(0, 0, T2 // 2, z_left)
         open_chunk(0)
         open_chunk(1)
-        sigmoid(2, 0, T2)
-        place(hs[(1, 3)], 3, 0, S)
-        for c in range(4):
-            sigmoid(3, c * BANK, (c + 1) * BANK)
 
         out_v = out.rearrange("(n p) c -> p n c", p=P)
 
         def finish_chunk(c):
-            res = big.tile([P, 4, BANK], F32, name="res", tag="big", align_bytes=64)
+            res = slot((6, 10, 11, 12)[c], [P, 4, BANK], F32, "res")
             for nt in range(4):
                 response_pass(accs[(nt, c)], 1, nt, c)
             for nt in range(4):
@@ -254,17 +331,13 @@ def tile_list_valve_command_response_kernel(
                     nc.vector.tensor_copy(out=res[:, nt, :], in_=accs[(nt, c)][:])
                 else:
                     nc.scalar.copy(out=res[:, nt, :], in_=accs[(nt, c)][:])
-                if nt % 2 == 1:
-                    nc.sync.dma_start(
-                        out=out_v[:, nt - 1 : nt + 1, c * BANK : (c + 1) * BANK],
-                        in_=res[:, nt - 1 : nt + 1, :],
-                    )
+                nc.sync.dma_start(out=out_v[:, nt, c * BANK : (c + 1) * BANK], in_=res[:, nt, :])
             if c + 2 < 4:
                 open_chunk(c + 2)
 
-        z_bf = [commands(1, 0)]
         for c in range(4):
-            if c + 1 < 4:
-                z_bf.append(commands(1, c + 1))
-            quantize_z(1, c, z_bf[c])
+            z_bf = commands(c)
+            if c == 0:
+                quantize_z(0, T2 // 2, T2, z_right)
+            quantize_z(1, c * BANK, (c + 1) * BANK, z_bf)
             finish_chunk(c)

@@ -21,8 +21,43 @@ P = 128
 PACK = 4
 KP = P * PACK
 BANK = 512
-QUADS = 4
+CHUNKS = T2 // BANK
+NT = N // P
 QP = 32
+QROWS = 4
+LIST_ROWS = 16
+QUADRANTS_BY_HALVES = (0, 2, 1, 3)
+
+W1_A0G0 = "w1_a0g0"
+W1_A1G0 = "w1_a1g0"
+W1_A0G1 = "w1_a0g1"
+W1_A1G1 = "w1_a1g1"
+TABLE_0 = "table_0"
+TABLE_1 = "table_1"
+GATE_2 = "gate_2"
+GATE_3 = "gate_3"
+GATE_CHUNK_2 = "gate_chunk_2"
+GATE_CHUNK_3 = "gate_chunk_3"
+ROUNDED_G0 = "rounded_g0"
+ROUNDED_A0G1 = "rounded_a0g1"
+ROUNDED_A1G1 = "rounded_a1g1"
+H_A = "h_a"
+H_B = "h_b"
+H_C = "h_c"
+H_D = "h_d"
+
+W1_BUFFER = {(0, 0): W1_A0G0, (1, 0): W1_A1G0, (0, 1): W1_A0G1, (1, 1): W1_A1G1}
+TABLE_BUFFER = (TABLE_0, TABLE_1)
+H_BUFFER = {
+    (0, 1): H_A, (0, 2): H_B, (0, 3): H_C, (1, 0): H_D, (1, 1): H_B, (1, 2): H_C, (1, 3): H_D,
+}
+OLD_ROWS_BUFFER = (W1_A0G0, W1_A1G0, W1_A1G1, TABLE_1)
+GATE_ROWS_BUFFER = (W1_A0G1, ROUNDED_A0G1, GATE_2, GATE_3)
+OLD_CHUNK_BUFFER = (TABLE_0, W1_A1G0, W1_A1G1, TABLE_1)
+GATE_CHUNK_BUFFER = (W1_A0G0, W1_A0G1, GATE_CHUNK_2, GATE_CHUNK_3)
+Z_CHUNK_BUFFER = (H_C, ROUNDED_G0, ROUNDED_G0, H_B)
+RIGHT_CODES_BUFFER = {2: TABLE_0, 3: W1_A1G0}
+RESULT_BUFFER = (GATE_2, GATE_3, W1_A0G0, W1_A0G1)
 
 
 def tile_list_valve_command_response_kernel(
@@ -31,95 +66,84 @@ def tile_list_valve_command_response_kernel(
     nc = tc.nc
     with ExitStack() as ctx:
         keep = ctx.enter_context(tc.tile_pool(name="keep", bufs=1))
-        slots = ctx.enter_context(tc.tile_pool(name="slots", bufs=1))
-        eight = ctx.enter_context(tc.tile_pool(name="eight", bufs=8))
+        shared = ctx.enter_context(tc.tile_pool(name="shared", bufs=1))
         psum = ctx.enter_context(tc.psum_pool(name="psum", bufs=8))
 
-        def slot(n, shape, dtype, name):
-            return slots.tile(shape, dtype, name=name, tag="slot%d" % n, align_bytes=64)
+        def tenant(buffer, shape, dtype, name):
+            return shared.tile(shape, dtype, name=name, tag=buffer, align_bytes=64)
 
-        idx = keep.tile([P, S // 16], U16, name="idx")
-        idx2 = keep.tile([P, S // 16], U16, name="idx2")
+        idx = keep.tile([P, S // LIST_ROWS], U16, name="idx")
+        idx2 = keep.tile([P, S // LIST_ROWS], U16, name="idx2")
         tab_s = keep.tile([P, T], U8, name="tab_s", align_bytes=64)
-        v_s = keep.tile([P, S], U8, name="v_s", align_bytes=64)
-        v_w = [keep.tile([P, S], U32, name="v_w%d" % a, align_bytes=64) for a in range(2)]
+        v_w = [keep.tile([P, S], U32, name="v_w0", align_bytes=64)]
         pages = [keep.tile([P, T2], F32, name="page%d" % i, align_bytes=64) for i in range(2)]
         bias = keep.tile([P, 2, PACK], F32, name="bias")
         wg = [keep.tile([P, S], F32, name="wg%d" % t) for t in range(PACK)]
-        w1_w = [keep.tile([P, 2 * KP], U32, name="w1_w%d" % g, align_bytes=64) for g in range(2)]
+        w1_w = [keep.tile([P, 2 * KP], U32, name="w1_w0", align_bytes=64)]
         w1_s = [keep.tile([P, 2 * KP], U8, name="w1_s%d" % g, align_bytes=64) for g in range(2)]
-        z_w = {1: keep.tile([P, T2], U32, name="z_w1", align_bytes=64)}
+        z_w1 = keep.tile([P, T2], U32, name="z_w1", align_bytes=64)
+        z_w = {(1, c): z_w1[:, c * BANK : (c + 1) * BANK] for c in range(CHUNKS)}
         z_s = [keep.tile([P, T2], U8, name="z_s%d" % g, align_bytes=64) for g in range(2)]
         w4_w = keep.tile([P, 2, 2 * N], U8, name="w4_w", align_bytes=64)
         w4_s = keep.tile([P, 2 * N], U8, name="w4_s", align_bytes=64)
 
-        nc.gpsimd.memset(tab_s[:].bitcast(U32), 0)
+        nc.vector.memset(tab_s[:].bitcast(U32), 0)
         for page in pages:
             nc.vector.memset(page[:], 0.0)
         nc.vector.memset(w4_s[:].bitcast(U32), 0)
-        for q in range(QUADS):
-            nc.gpsimd.dma_start(
-                out=tab_s[QP * q : QP * q + 8, :].bitcast(I32),
-                in_=tab_scales[:, 4 * q : 4 * q + 4, :].bitcast(I32),
-            )
+
+        old_dealt = old.rearrange("(g p t) c -> g p t c", g=2, t=PACK)
+        wgs_dealt = wgs.rearrange("(q t) j -> q t j", t=PACK)
+        out_tiles = out.rearrange("(n p) c -> p n c", p=P)
 
         def load_w1(a, g):
-            raw = slot((1, 4)[g] + a, [P, PACK, KP], F32, "raw")
+            raw = tenant(W1_BUFFER[(a, g)], [P, PACK, KP], F32, "raw")
             rows = w1[a * KP : (a + 1) * KP, g * KP : (g + 1) * KP]
             nc.sync.dma_start(out=raw[:], in_=rows.rearrange("(p i) c -> p i c", i=PACK))
             return raw
 
-        old_dealt = old.rearrange("(g p t) c -> g p t c", g=2, t=PACK)
-
         def load_old_rows(t):
-            tile = slot(t, [P, T2], F32, "old_rows")
+            tile = tenant(OLD_ROWS_BUFFER[t], [P, T2], F32, "old_rows")
             nc.sync.dma_start(out=tile[:], in_=old_dealt[0, :, t, :])
             return tile
 
         def load_old_chunk(c):
-            tile = slot((4, 1, 2, 3)[c], [P, PACK, BANK], F32, "old_chunk")
+            tile = tenant(OLD_CHUNK_BUFFER[c], [P, PACK, BANK], F32, "old_chunk")
             nc.sync.dma_start(out=tile[:], in_=old_dealt[1, :, :, c * BANK : (c + 1) * BANK])
             return tile
 
         def load_table_words(a):
-            tile = slot(3 * a, [P, T], U32, "tab_w")
+            tile = tenant(TABLE_BUFFER[a], [P, T], U32, "tab_w")
             nc.sync.dma_start(
                 out=tile[:].bitcast(I32),
                 in_=tab_words[a].rearrange("p t i -> p (t i)").bitcast(I32),
             )
             return tile
 
-        wgs_dealt = wgs.rearrange("(q t) j -> q t j", t=PACK)
-
         def load_wg(t):
-            for q in range(QUADS):
+            for q in QUADRANTS_BY_HALVES:
                 nc.sync.dma_start(out=wg[t][QP * q : QP * (q + 1), :], in_=wgs_dealt[:, t, :])
 
-        nc.sync.dma_start(idx[:], offs)
-        tab_w = [load_table_words(0)]
-        w1_raw = {(0, 0): load_w1(0, 0), (1, 0): load_w1(1, 0)}
-        tab_w.append(load_table_words(1))
-        nc.sync.dma_start(idx2[:], offs2)
-        nc.sync.dma_start(out=bias[:], in_=b.rearrange("(g p t) -> p g t", g=2, t=PACK))
-        load_wg(0)
-        load_wg(1)
-        for a in range(2):
-            w1_raw[(a, 1)] = load_w1(a, 1)
-        load_wg(2)
-        load_wg(3)
+        def round_w1(a, g, rounded, slices, on_vector):
+            dst = rounded.rearrange("p (t m i) -> p m i t", t=PACK, i=PACK)
+            src = w1_raw[(a, g)][:].rearrange("p i (m t) -> p m i t", t=PACK)
+            for t in slices[::2]:
+                if on_vector:
+                    nc.vector.tensor_copy(out=dst[:, :, :, t : t + 2], in_=src[:, :, :, t : t + 2])
+                else:
+                    nc.scalar.activation(
+                        out=dst[:, :, :, t : t + 2], in_=src[:, :, :, t : t + 2], func=ACT.Copy
+                    )
 
-        def round_w1(a, g, grouped, on_vector, lo=0, hi=P):
-            dst = grouped[:, a, :].rearrange("p (t m i) -> p m i t", t=PACK, i=PACK)[:, lo:hi]
-            src = w1_raw[(a, g)][:].rearrange("p i (m t) -> p m i t", t=PACK)[:, lo:hi]
-            if on_vector:
-                nc.vector.tensor_copy(out=dst, in_=src)
-            else:
-                nc.scalar.activation(out=dst, in_=src, func=ACT.Copy)
+        def quantize_w1(a, g, rounded):
+            cols = slice(a * KP, (a + 1) * KP)
+            nc.vector.quantize_mx(
+                out=w1_w[g][:, cols].bitcast(FP8X4), scales=w1_s[g][:, cols], in_=rounded
+            )
 
         def gather_words(a, lo, hi):
-            nc.vector.tensor_copy(
-                out=v_w[a][:, lo:hi], in_=tab_w[a][:].indirect(idx[:, lo // 16 : hi // 16])
-            )
+            entries = idx[:, lo // LIST_ROWS : hi // LIST_ROWS]
+            nc.vector.tensor_copy(out=v_w[a][:, lo:hi], in_=tab_w[a][:].indirect(entries))
 
         def first_product(g, t, half):
             cols = slice(half * BANK, (half + 1) * BANK)
@@ -131,154 +155,217 @@ def tile_list_valve_command_response_kernel(
                     lhsT=w1_w[g][:, m].bitcast(FP8X4),
                     lhsT_scale=w1_s[g][:, m],
                     rhs=v_w[a][:, cols].bitcast(FP8X4),
-                    rhs_scale=v_s[4 * a : P, cols],
+                    rhs_scale=v_s[QROWS * a : P, cols],
                     start=(a == 0),
                     stop=(a == 1),
                 )
             return acc
 
+        def add_bias(h, g, t, half):
+            nc.scalar.activation(
+                out=h[:, half * BANK : (half + 1) * BANK],
+                in_=first_product(g, t, half)[:],
+                func=ACT.Identity,
+                bias=bias[:, g, t : t + 1],
+            )
+
         def signals(g, t):
-            h = eight.tile([P, S], F32, name="h", tag="H", align_bytes=64)
+            h = tenant(H_BUFFER[(g, t)], [P, S], F32, "h")
             for half in range(2):
-                acc = first_product(g, t, half)
-                nc.scalar.activation(
-                    out=h[:, half * BANK : (half + 1) * BANK],
-                    in_=acc[:],
-                    func=ACT.Identity,
-                    bias=bias[:, g, t : t + 1],
-                )
+                add_bias(h, g, t, half)
             return h
 
-        def weigh(dst, h, t):
-            nc.gpsimd.tensor_tensor(dst, h[:], wg[t][:], MULT)
+        def weigh(h, t, lo=0, hi=S):
+            nc.gpsimd.tensor_tensor(h[:, lo:hi], h[:, lo:hi], wg[t][:, lo:hi], MULT)
 
-        def place(src, t, lo, hi):
-            nc.vector.tensor_copy(pages[t % 2][:].indirect(idx2[:, lo // 16 : hi // 16]), src)
-
-        gather_words(0, 0, S)
-        nc.vector.tensor_copy(out=v_s[:], in_=tab_s[:].indirect(idx[:]))
-        w1_bf = slot(12, [P, 2, KP * PACK], BF16, "w1_bf")
-        round_w1(0, 0, w1_bf, False)
-        round_w1(1, 0, w1_bf, True, 0, P // 2)
-        round_w1(1, 0, w1_bf, False, P // 2, P)
-        for a in range(2):
-            nc.vector.quantize_mx(
-                out=w1_w[0][:, a * KP : (a + 1) * KP].bitcast(FP8X4),
-                scales=w1_s[0][:, a * KP : (a + 1) * KP],
-                in_=w1_bf[:, a, :],
-            )
-        gather_words(1, 0, BANK)
-        gather_words(1, BANK, S)
-
-        h_first = eight.tile([P, S], F32, name="h", tag="H", align_bytes=64)
-        for half in range(2):
-            cols = slice(half * BANK, (half + 1) * BANK)
-            acc = first_product(0, 0, half)
-            nc.vector.scalar_tensor_tensor(
-                out=h_first[:, cols],
-                in0=acc[:],
-                scalar=bias[:, 0, 0:1],
-                in1=wg[0][:, cols],
-                op0=ADD,
-                op1=MULT,
-            )
-            place(h_first[:, cols], 0, half * BANK, (half + 1) * BANK)
-        hs = {(0, t): signals(0, t) for t in range(1, PACK)}
-        for t in range(1, PACK):
-            weigh(hs[(0, t)][:], hs[(0, t)], t)
-
-        w1_bf = slot(13, [P, 2, KP * PACK], BF16, "w1_bf")
-        for a in range(2):
-            round_w1(a, 1, w1_bf, False)
-        old_rows = [load_old_rows(t) for t in range(PACK)]
-        nc.sync.dma_start(
-            out=w4_w[:].bitcast(I32), in_=w4_words.rearrange("a p e -> p a e").bitcast(I32)
-        )
-        for q in range(QUADS):
-            nc.sync.dma_start(
-                out=w4_s[QP * q : QP * q + 4, :].rearrange("r (a n) -> r a n", a=2).bitcast(I32),
-                in_=w4_scales[:, 4 * q : 4 * q + 4, :].rearrange("a r n -> r a n").bitcast(I32),
-            )
-
-        z_rows = [slot(10 + half, [P, PACK, T2 // 2], BF16, "z_rows") for half in range(2)]
+        def place(h, t, lo=0, hi=S):
+            entries = idx2[:, lo // LIST_ROWS : hi // LIST_ROWS]
+            nc.vector.tensor_copy(pages[t % 2][:].indirect(entries), h[:, lo:hi])
 
         def gate_rows(t):
-            gate = slot((5, 13, 6, 7)[t], [P, T2], F32, "gate_rows")
+            gate = tenant(GATE_ROWS_BUFFER[t], [P, T2], F32, "gate_rows")
             nc.scalar.activation(out=gate[:], in_=pages[t % 2][:], func=ACT.Sigmoid)
             return gate
 
-        def commands_rows(t, gate):
-            for half in range(2):
-                cols = slice(half * (T2 // 2), (half + 1) * (T2 // 2))
-                nc.gpsimd.tensor_tensor(
-                    z_rows[half][:, t, :], old_rows[t][:, cols], gate[:, cols], MULT
-                )
-
-        gate = [gate_rows(0)]
-        place(hs[(0, 1)][:], 1, 0, S)
-        nc.vector.quantize_mx(
-            out=w1_w[1][:].bitcast(FP8X4),
-            scales=w1_s[1][:],
-            in_=w1_bf[:].rearrange("p a e -> p (a e)"),
-        )
-        for t in range(PACK):
-            hs[(1, t)] = signals(1, t)
-        for t in range(2):
-            weigh(hs[(1, t)][:], hs[(1, t)], t)
-        commands_rows(0, gate[0])
-        gate.append(gate_rows(1))
-        place(hs[(0, 2)][:], 2, 0, S)
-        commands_rows(1, gate[1])
-        gate.append(gate_rows(2))
-        place(hs[(0, 3)][:], 3, 0, S)
-        commands_rows(2, gate[2])
-        late = {2: slot(6, [P, S], F32, "late")}
-        weigh(late[2][:], hs[(1, 2)], 2)
-        gate.append(gate_rows(3))
-        place(hs[(1, 0)][:], 0, 0, S)
-        commands_rows(3, gate[3])
-        late[3] = slot(7, [P, S], F32, "late")
-        weigh(late[3][:], hs[(1, 3)], 3)
-        old_chunks = [load_old_chunk(c) for c in range(4)]
-
-        gates = [slot((0, 5, 8, 9)[c], [P, PACK, BANK], F32, "gate_chunk") for c in range(4)]
-
-        def sigmoid(t):
-            for c in range(4):
+        def gate_chunks(t):
+            for c in range(CHUNKS):
                 nc.scalar.activation(
                     out=gates[c][:, t, :],
                     in_=pages[t % 2][:, c * BANK : (c + 1) * BANK],
                     func=ACT.Sigmoid,
                 )
 
-        def interleave(half):
-            z_bf = slot(12 + half, [P, T2 // 2 * PACK], BF16, "z_bf0")
-            for part in range(2):
-                dst = z_bf[:, part * BANK * PACK : (part + 1) * BANK * PACK]
-                src = z_rows[half][:, :, part * BANK : (part + 1) * BANK]
-                if half == 0:
-                    nc.gpsimd.tensor_scalar(
-                        dst.rearrange("p (c t) -> p c t", t=PACK),
-                        src.rearrange("p t c -> p c t"),
-                        1.0,
-                        0.0,
-                        MULT,
-                        ADD,
-                    )
-                else:
-                    nc.scalar.copy(
-                        out=dst.rearrange("p (c i t) -> p c t i", i=4, t=PACK),
-                        in_=src.rearrange("p t (c i) -> p c t i", i=4),
-                    )
-            return z_bf
-
-        def quantize_z(g, lo, hi, z_bf):
-            nc.vector.quantize_mx(
-                out=z_w[g][:, lo:hi].bitcast(FP8X4), scales=z_s[g][:, lo:hi], in_=z_bf[:]
+        def interleave_on_scalar(dst, rows):
+            nc.scalar.copy(
+                out=dst.rearrange("p (c i t) -> p c t i", i=4, t=PACK),
+                in_=rows.rearrange("p t (c i) -> p c t i", i=4),
             )
 
+        def quantize_z(g, lo, hi, codes, z_bf):
+            nc.vector.quantize_mx(out=codes.bitcast(FP8X4), scales=z_s[g][:, lo:hi], in_=z_bf)
+
+        def response_pass(g, nt, c):
+            nc.tensor.matmul_mx(
+                out=accs[(nt, c)][:],
+                lhsT=w4_w[:, g, 2 * P * nt : 2 * P * (nt + 1)].bitcast(FP4X4),
+                lhsT_scale=w4_s[:, g * N + P * nt : g * N + P * (nt + 1)],
+                rhs=z_w[(g, c)].bitcast(FP8X4),
+                rhs_scale=z_s[g][:, c * BANK : (c + 1) * BANK],
+                start=(g == 0),
+                stop=(g == 1),
+            )
+
+        def open_chunk(c):
+            for nt in range(NT):
+                accs[(nt, c)] = psum.tile([P, BANK], F32, name="acc", tag="acc")
+                response_pass(0, nt, c)
+
+        def finish_chunk(c):
+            res = tenant(RESULT_BUFFER[c], [P, NT, BANK], F32, "res")
+            for nt in range(NT):
+                response_pass(1, nt, c)
+            for nt in range(NT):
+                if c == CHUNKS - 1 and nt % 2 == 1:
+                    nc.vector.tensor_copy(out=res[:, nt, :], in_=accs[(nt, c)][:])
+                else:
+                    nc.scalar.copy(out=res[:, nt, :], in_=accs[(nt, c)][:])
+                nc.sync.dma_start(
+                    out=out_tiles[:, nt, c * BANK : (c + 1) * BANK], in_=res[:, nt, :]
+                )
+
+        nc.sync.dma_start(idx[:], offs)
+        for q in QUADRANTS_BY_HALVES:
+            nc.sync.dma_start(
+                out=tab_s[QP * q : QP * q + 2 * QROWS, :].bitcast(I32),
+                in_=tab_scales[:, QROWS * q : QROWS * (q + 1), :].bitcast(I32),
+            )
+        tab_w = [load_table_words(0)]
+        w1_raw = {(a, 0): load_w1(a, 0) for a in range(2)}
+        tab_w.append(load_table_words(1))
+        nc.sync.dma_start(idx2[:], offs2)
+        nc.sync.dma_start(out=bias[:], in_=b.rearrange("(g p t) -> p g t", g=2, t=PACK))
+        load_wg(0)
+        load_wg(1)
+        w1_raw[(1, 1)] = load_w1(1, 1)
+
+        gather_words(0, 0, S)
+        v_s = tenant(TABLE_0, [P, S], U8, "v_s")
+        nc.vector.tensor_copy(out=v_s[:], in_=tab_s[:].indirect(idx[:]))
+        rounded_g0 = tenant(ROUNDED_G0, [P, 2, KP * PACK], BF16, "rounded_g0")
+        round_w1(0, 0, rounded_g0[:, 0, :], range(PACK), on_vector=False)
+        round_w1(1, 0, rounded_g0[:, 1, :], range(0, 2), on_vector=True)
+        round_w1(1, 0, rounded_g0[:, 1, :], range(2, PACK), on_vector=False)
+        for a in range(2):
+            quantize_w1(a, 0, rounded_g0[:, a, :])
+        v_w.append(tenant(ROUNDED_G0, [P, S], U32, "v_w1"))
+        for half in range(2):
+            gather_words(1, half * BANK, (half + 1) * BANK)
+
+        load_wg(2)
+        load_wg(3)
+        w1_raw[(0, 1)] = load_w1(0, 1)
+
+        h_first = keep.tile([P, S], F32, name="h_first", align_bytes=64)
+        nc.vector.scalar_tensor_tensor(
+            out=h_first[:, 0:BANK],
+            in0=first_product(0, 0, 0)[:],
+            scalar=bias[:, 0, 0:1],
+            in1=wg[0][:, 0:BANK],
+            op0=ADD,
+            op1=MULT,
+        )
+        place(h_first, 0, 0, BANK)
+        add_bias(h_first, 0, 0, 1)
+        weigh(h_first, 0, BANK, S)
+        place(h_first, 0, BANK, S)
+        hs = {(0, t): signals(0, t) for t in range(1, PACK)}
+        for t in range(1, PACK):
+            weigh(hs[(0, t)], t)
+
+        rounded_g1 = [
+            tenant(buffer, [P, KP * PACK], BF16, "rounded_g1")
+            for buffer in (ROUNDED_A0G1, ROUNDED_A1G1)
+        ]
+        for a in (1, 0):
+            round_w1(a, 1, rounded_g1[a][:], range(PACK), on_vector=False)
+        old_rows = [load_old_rows(t) for t in range(PACK)]
+        nc.sync.dma_start(
+            out=w4_w[:].bitcast(I32), in_=w4_words.rearrange("a p e -> p a e").bitcast(I32)
+        )
+        for q in range(P // QP):
+            nc.sync.dma_start(
+                out=w4_s[QP * q : QP * q + QROWS, :].rearrange("r (a n) -> r a n", a=2).bitcast(I32),
+                in_=w4_scales[:, QROWS * q : QROWS * (q + 1), :]
+                .rearrange("a r n -> r a n")
+                .bitcast(I32),
+            )
+
+        place(hs[(0, 1)], 1)
+        gate = gate_rows(0)
+        w1_w.append(tenant(H_A, [P, 2 * KP], U32, "w1_w1"))
+        for a in (1, 0):
+            quantize_w1(a, 1, rounded_g1[a][:])
+
+        z_rows = tenant(ROUNDED_A1G1, [P, PACK, T2], BF16, "z_rows")
+        nc.gpsimd.tensor_tensor(z_rows[:, 0, :], old_rows[0][:], gate[:], MULT)
+        place(hs[(0, 2)], 2)
+        hs[(1, 0)] = signals(1, 0)
+        weigh(hs[(1, 0)], 0)
+        next_to_place = {1: (0, 3), 2: (1, 0)}
+        for t in range(1, PACK):
+            gate = gate_rows(t)
+            hs[(1, t)] = signals(1, t)
+            weigh(hs[(1, t)], t)
+            nc.gpsimd.tensor_tensor(z_rows[:, t, :], old_rows[t][:], gate[:], MULT)
+            if t in next_to_place:
+                place(hs[next_to_place[t]], next_to_place[t][1])
+
+        old_chunks = [load_old_chunk(c) for c in range(CHUNKS)]
+        gates = [
+            tenant(GATE_CHUNK_BUFFER[c], [P, PACK, BANK], F32, "gate_chunk") for c in range(CHUNKS)
+        ]
+        for t in range(2):
+            place(hs[(1, t + 1)], t + 1)
+            gate_chunks(t)
+
+        z_left = tenant(ROUNDED_G0, [P, 2 * BANK * PACK], BF16, "z_left")
+        nc.gpsimd.tensor_scalar(
+            z_left[:].rearrange("p (c t) -> p c t", t=PACK),
+            z_rows[:, :, 0 : 2 * BANK].rearrange("p t c -> p c t"),
+            1.0,
+            0.0,
+            MULT,
+            ADD,
+        )
+        z_right = tenant(H_B, [P, 2 * BANK * PACK], BF16, "z_right")
+        right_part = {
+            c: z_right[:, (c - 2) * BANK * PACK : (c - 1) * BANK * PACK] for c in range(2, CHUNKS)
+        }
+        for c in range(2, CHUNKS):
+            interleave_on_scalar(right_part[c], z_rows[:, :, c * BANK : (c + 1) * BANK])
+
+        early_rows = tenant(H_A, [P, PACK, BANK], BF16, "early_rows")
+        nc.gpsimd.tensor_tensor(
+            early_rows[:, 0:2, :], old_chunks[0][:, 0:2, :], gates[0][:, 0:2, :], MULT
+        )
+        place(hs[(1, 3)], 3)
+        gate_chunks(2)
+        nc.gpsimd.tensor_tensor(early_rows[:, 2, :], old_chunks[0][:, 2, :], gates[0][:, 2, :], MULT)
+        gate_chunks(3)
+
+        accs = {}
+        left_codes = tenant(H_D, [P, 2 * BANK], U32, "z_w0")
+        quantize_z(0, 0, 2 * BANK, left_codes[:], z_left[:])
+        for c in (1, 0):
+            z_w[(0, c)] = left_codes[:, c * BANK : (c + 1) * BANK]
+            open_chunk(c)
+
+        nc.vector.tensor_tensor(early_rows[:, 3, :], old_chunks[0][:, 3, :], gates[0][:, 3, :], MULT)
+        z_early = tenant(Z_CHUNK_BUFFER[0], [P, BANK * PACK], BF16, "z_early")
+        interleave_on_scalar(z_early[:], early_rows[:])
+
         def commands(c):
-            z_bf = eight.tile([P, BANK * PACK], BF16, name="z_bf1", tag="H", align_bytes=64)
+            z_bf = tenant(Z_CHUNK_BUFFER[c], [P, BANK * PACK], BF16, "z_bf")
             nc.vector.tensor_tensor(
                 z_bf[:].rearrange("p (c i t) -> p c t i", i=2, t=PACK),
                 old_chunks[c][:].rearrange("p t (c i) -> p c t i", i=2),
@@ -287,57 +374,21 @@ def tile_list_valve_command_response_kernel(
             )
             return z_bf
 
-        def response_pass(acc, g, nt, c):
-            cols = slice(c * BANK, (c + 1) * BANK)
-            nc.tensor.matmul_mx(
-                out=acc[:],
-                lhsT=w4_w[:, g, 2 * P * nt : 2 * P * (nt + 1)].bitcast(FP4X4),
-                lhsT_scale=w4_s[:, g * N + P * nt : g * N + P * (nt + 1)],
-                rhs=z_w[g][:, cols].bitcast(FP8X4),
-                rhs_scale=z_s[g][:, cols],
-                start=(g == 0),
-                stop=(g == 1),
-            )
+        def quantize_right(c):
+            z_w[(0, c)] = tenant(RIGHT_CODES_BUFFER[c], [P, BANK], U32, "z_w0")[:]
+            quantize_z(0, c * BANK, (c + 1) * BANK, z_w[(0, c)], right_part[c])
 
-        accs = {}
-
-        def open_chunk(c):
-            for nt in range(4):
-                accs[(nt, c)] = psum.tile([P, BANK], F32, name="acc", tag="acc")
-                response_pass(accs[(nt, c)], 0, nt, c)
-
-        sigmoid(0)
-        place(hs[(1, 1)][:], 1, 0, S)
-        sigmoid(1)
-        place(late[2][:], 2, 0, S)
-        z_left = interleave(0)
-        z_right = interleave(1)
-        sigmoid(2)
-        place(late[3][:], 3, 0, S)
-        sigmoid(3)
-        z_w[0] = slot(7, [P, T2], U32, "z_w0")
-        quantize_z(0, 0, T2 // 2, z_left)
-        open_chunk(0)
-        open_chunk(1)
-
-        out_v = out.rearrange("(n p) c -> p n c", p=P)
-
-        def finish_chunk(c):
-            res = slot((6, 10, 11, 12)[c], [P, 4, BANK], F32, "res")
-            for nt in range(4):
-                response_pass(accs[(nt, c)], 1, nt, c)
-            for nt in range(4):
-                if c == 3 and nt % 2 == 1:
-                    nc.vector.tensor_copy(out=res[:, nt, :], in_=accs[(nt, c)][:])
-                else:
-                    nc.scalar.copy(out=res[:, nt, :], in_=accs[(nt, c)][:])
-                nc.sync.dma_start(out=out_v[:, nt, c * BANK : (c + 1) * BANK], in_=res[:, nt, :])
-            if c + 2 < 4:
-                open_chunk(c + 2)
-
-        for c in range(4):
-            z_bf = commands(c)
-            if c == 0:
-                quantize_z(0, T2 // 2, T2, z_right)
-            quantize_z(1, c * BANK, (c + 1) * BANK, z_bf)
+        def respond(c, z_bf):
+            quantize_z(1, c * BANK, (c + 1) * BANK, z_w[(1, c)], z_bf[:])
             finish_chunk(c)
+
+        z_bf = commands(1)
+        quantize_right(2)
+        respond(1, z_bf)
+        respond(0, z_early)
+        open_chunk(2)
+        z_bf = commands(2)
+        quantize_right(3)
+        open_chunk(3)
+        respond(2, z_bf)
+        respond(3, commands(3))

from contextlib import ExitStack

import concourse.mybir as mybir

K, T, S, H, T2, N = 1024, 2048, 1024, 1024, 2048, 512
FLOPS = 2 * K * H * S + 2 * H * N * T2

F32 = mybir.dt.float32
BF16 = mybir.dt.bfloat16
I32 = mybir.dt.int32
U32 = mybir.dt.uint32
U16 = mybir.dt.uint16
U8 = mybir.dt.uint8
FP8X4 = mybir.dt.float8_e4m3fn_x4
FP4X4 = mybir.dt.float4_e2m1fn_x4
ACT = mybir.ActivationFunctionType
MULT = mybir.AluOpType.mult
ADD = mybir.AluOpType.add

P = 128
PACK = 4
KP = P * PACK
BANK = 512
CHUNKS = T2 // BANK
NT = N // P
QP = 32
QROWS = 4
LIST_ROWS = 16
QUADRANTS_BY_HALVES = (0, 2, 1, 3)

W1_A0G0 = "w1_a0g0"
W1_A1G0 = "w1_a1g0"
W1_A0G1 = "w1_a0g1"
W1_A1G1 = "w1_a1g1"
TABLE_0 = "table_0"
TABLE_1 = "table_1"
GATE_2 = "gate_2"
GATE_3 = "gate_3"
GATE_CHUNK_2 = "gate_chunk_2"
GATE_CHUNK_3 = "gate_chunk_3"
ROUNDED_G0 = "rounded_g0"
ROUNDED_A0G1 = "rounded_a0g1"
ROUNDED_A1G1 = "rounded_a1g1"
H_A = "h_a"
H_B = "h_b"
H_C = "h_c"
H_D = "h_d"

W1_BUFFER = {(0, 0): W1_A0G0, (1, 0): W1_A1G0, (0, 1): W1_A0G1, (1, 1): W1_A1G1}
TABLE_BUFFER = (TABLE_0, TABLE_1)
H_BUFFER = {
    (0, 1): H_A, (0, 2): H_B, (0, 3): H_C, (1, 0): H_D, (1, 1): H_B, (1, 2): H_C, (1, 3): H_D,
}
OLD_ROWS_BUFFER = (W1_A0G0, W1_A1G0, W1_A1G1, TABLE_1)
GATE_ROWS_BUFFER = (W1_A0G1, ROUNDED_A0G1, GATE_2, GATE_3)
OLD_CHUNK_BUFFER = (TABLE_0, W1_A1G0, W1_A1G1, TABLE_1)
GATE_CHUNK_BUFFER = (W1_A0G0, W1_A0G1, GATE_CHUNK_2, GATE_CHUNK_3)
Z_CHUNK_BUFFER = (H_C, ROUNDED_G0, ROUNDED_G0, H_B)
RIGHT_CODES_BUFFER = {2: TABLE_0, 3: W1_A1G0}
RESULT_BUFFER = (GATE_2, GATE_3, W1_A0G0, W1_A0G1)


def tile_list_valve_command_response_kernel(
    tc, tab_words, tab_scales, offs, w1, b, offs2, wgs, old, w4_words, w4_scales, out
):
    nc = tc.nc
    with ExitStack() as ctx:
        keep = ctx.enter_context(tc.tile_pool(name="keep", bufs=1))
        shared = ctx.enter_context(tc.tile_pool(name="shared", bufs=1))
        psum = ctx.enter_context(tc.psum_pool(name="psum", bufs=8))

        def tenant(buffer, shape, dtype, name):
            return shared.tile(shape, dtype, name=name, tag=buffer, align_bytes=64)

        idx = keep.tile([P, S // LIST_ROWS], U16, name="idx")
        idx2 = keep.tile([P, S // LIST_ROWS], U16, name="idx2")
        tab_s = keep.tile([P, T], U8, name="tab_s", align_bytes=64)
        v_w = [keep.tile([P, S], U32, name="v_w0", align_bytes=64)]
        pages = [keep.tile([P, T2], F32, name="page%d" % i, align_bytes=64) for i in range(2)]
        bias = keep.tile([P, 2, PACK], F32, name="bias")
        wg = [keep.tile([P, S], F32, name="wg%d" % t) for t in range(PACK)]
        w1_w = [keep.tile([P, 2 * KP], U32, name="w1_w0", align_bytes=64)]
        w1_s = [keep.tile([P, 2 * KP], U8, name="w1_s%d" % g, align_bytes=64) for g in range(2)]
        z_w1 = keep.tile([P, T2], U32, name="z_w1", align_bytes=64)
        z_w = {(1, c): z_w1[:, c * BANK : (c + 1) * BANK] for c in range(CHUNKS)}
        z_s = [keep.tile([P, T2], U8, name="z_s%d" % g, align_bytes=64) for g in range(2)]
        w4_w = keep.tile([P, 2, 2 * N], U8, name="w4_w", align_bytes=64)
        w4_s = keep.tile([P, 2 * N], U8, name="w4_s", align_bytes=64)

        nc.vector.memset(tab_s[:].bitcast(U32), 0)
        for page in pages:
            nc.vector.memset(page[:], 0.0)
        nc.vector.memset(w4_s[:].bitcast(U32), 0)

        old_dealt = old.rearrange("(g p t) c -> g p t c", g=2, t=PACK)
        wgs_dealt = wgs.rearrange("(q t) j -> q t j", t=PACK)
        out_tiles = out.rearrange("(n p) c -> p n c", p=P)

        def load_w1(a, g):
            raw = tenant(W1_BUFFER[(a, g)], [P, PACK, KP], F32, "raw")
            rows = w1[a * KP : (a + 1) * KP, g * KP : (g + 1) * KP]
            nc.sync.dma_start(out=raw[:], in_=rows.rearrange("(p i) c -> p i c", i=PACK))
            return raw

        def load_old_rows(t):
            tile = tenant(OLD_ROWS_BUFFER[t], [P, T2], F32, "old_rows")
            nc.sync.dma_start(out=tile[:], in_=old_dealt[0, :, t, :])
            return tile

        def load_old_chunk(c):
            tile = tenant(OLD_CHUNK_BUFFER[c], [P, PACK, BANK], F32, "old_chunk")
            nc.sync.dma_start(out=tile[:], in_=old_dealt[1, :, :, c * BANK : (c + 1) * BANK])
            return tile

        def load_table_words(a):
            tile = tenant(TABLE_BUFFER[a], [P, T], U32, "tab_w")
            nc.sync.dma_start(
                out=tile[:].bitcast(I32),
                in_=tab_words[a].rearrange("p t i -> p (t i)").bitcast(I32),
            )
            return tile

        def load_wg(t):
            for q in QUADRANTS_BY_HALVES:
                nc.sync.dma_start(out=wg[t][QP * q : QP * (q + 1), :], in_=wgs_dealt[:, t, :])

        def round_w1(a, g, rounded, slices, on_vector):
            dst = rounded.rearrange("p (t m i) -> p m i t", t=PACK, i=PACK)
            src = w1_raw[(a, g)][:].rearrange("p i (m t) -> p m i t", t=PACK)
            for t in slices[::2]:
                if on_vector:
                    nc.vector.tensor_copy(out=dst[:, :, :, t : t + 2], in_=src[:, :, :, t : t + 2])
                else:
                    nc.scalar.activation(
                        out=dst[:, :, :, t : t + 2], in_=src[:, :, :, t : t + 2], func=ACT.Copy
                    )

        def quantize_w1(a, g, rounded):
            cols = slice(a * KP, (a + 1) * KP)
            nc.vector.quantize_mx(
                out=w1_w[g][:, cols].bitcast(FP8X4), scales=w1_s[g][:, cols], in_=rounded
            )

        def gather_words(a, lo, hi):
            entries = idx[:, lo // LIST_ROWS : hi // LIST_ROWS]
            nc.vector.tensor_copy(out=v_w[a][:, lo:hi], in_=tab_w[a][:].indirect(entries))

        def first_product(g, t, half):
            cols = slice(half * BANK, (half + 1) * BANK)
            acc = psum.tile([P, BANK], F32, name="acc", tag="acc")
            for a in range(2):
                m = slice(a * KP + t * P, a * KP + (t + 1) * P)
                nc.tensor.matmul_mx(
                    out=acc[:],
                    lhsT=w1_w[g][:, m].bitcast(FP8X4),
                    lhsT_scale=w1_s[g][:, m],
                    rhs=v_w[a][:, cols].bitcast(FP8X4),
                    rhs_scale=v_s[QROWS * a : P, cols],
                    start=(a == 0),
                    stop=(a == 1),
                )
            return acc

        def add_bias(h, g, t, half):
            nc.scalar.activation(
                out=h[:, half * BANK : (half + 1) * BANK],
                in_=first_product(g, t, half)[:],
                func=ACT.Identity,
                bias=bias[:, g, t : t + 1],
            )

        def signals(g, t):
            h = tenant(H_BUFFER[(g, t)], [P, S], F32, "h")
            for half in range(2):
                add_bias(h, g, t, half)
            return h

        def weigh(h, t, lo=0, hi=S):
            nc.gpsimd.tensor_tensor(h[:, lo:hi], h[:, lo:hi], wg[t][:, lo:hi], MULT)

        def place(h, t, lo=0, hi=S):
            entries = idx2[:, lo // LIST_ROWS : hi // LIST_ROWS]
            nc.vector.tensor_copy(pages[t % 2][:].indirect(entries), h[:, lo:hi])

        def gate_rows(t):
            gate = tenant(GATE_ROWS_BUFFER[t], [P, T2], F32, "gate_rows")
            nc.scalar.activation(out=gate[:], in_=pages[t % 2][:], func=ACT.Sigmoid)
            return gate

        def gate_chunks(t):
            for c in range(CHUNKS):
                nc.scalar.activation(
                    out=gates[c][:, t, :],
                    in_=pages[t % 2][:, c * BANK : (c + 1) * BANK],
                    func=ACT.Sigmoid,
                )

        def interleave_on_scalar(dst, rows):
            nc.scalar.copy(
                out=dst.rearrange("p (c i t) -> p c t i", i=4, t=PACK),
                in_=rows.rearrange("p t (c i) -> p c t i", i=4),
            )

        def quantize_z(g, lo, hi, codes, z_bf):
            nc.vector.quantize_mx(out=codes.bitcast(FP8X4), scales=z_s[g][:, lo:hi], in_=z_bf)

        def response_pass(g, nt, c):
            nc.tensor.matmul_mx(
                out=accs[(nt, c)][:],
                lhsT=w4_w[:, g, 2 * P * nt : 2 * P * (nt + 1)].bitcast(FP4X4),
                lhsT_scale=w4_s[:, g * N + P * nt : g * N + P * (nt + 1)],
                rhs=z_w[(g, c)].bitcast(FP8X4),
                rhs_scale=z_s[g][:, c * BANK : (c + 1) * BANK],
                start=(g == 0),
                stop=(g == 1),
            )

        def open_chunk(c):
            for nt in range(NT):
                accs[(nt, c)] = psum.tile([P, BANK], F32, name="acc", tag="acc")
                response_pass(0, nt, c)

        def finish_chunk(c):
            res = tenant(RESULT_BUFFER[c], [P, NT, BANK], F32, "res")
            for nt in range(NT):
                response_pass(1, nt, c)
            for nt in range(NT):
                if c == CHUNKS - 1 and nt % 2 == 1:
                    nc.vector.tensor_copy(out=res[:, nt, :], in_=accs[(nt, c)][:])
                else:
                    nc.scalar.copy(out=res[:, nt, :], in_=accs[(nt, c)][:])
                nc.sync.dma_start(
                    out=out_tiles[:, nt, c * BANK : (c + 1) * BANK], in_=res[:, nt, :]
                )

        nc.sync.dma_start(idx[:], offs)
        for q in QUADRANTS_BY_HALVES:
            nc.sync.dma_start(
                out=tab_s[QP * q : QP * q + 2 * QROWS, :].bitcast(I32),
                in_=tab_scales[:, QROWS * q : QROWS * (q + 1), :].bitcast(I32),
            )
        tab_w = [load_table_words(0)]
        w1_raw = {(a, 0): load_w1(a, 0) for a in range(2)}
        tab_w.append(load_table_words(1))
        nc.sync.dma_start(idx2[:], offs2)
        nc.sync.dma_start(out=bias[:], in_=b.rearrange("(g p t) -> p g t", g=2, t=PACK))
        load_wg(0)
        load_wg(1)
        w1_raw[(1, 1)] = load_w1(1, 1)

        gather_words(0, 0, S)
        v_s = tenant(TABLE_0, [P, S], U8, "v_s")
        nc.vector.tensor_copy(out=v_s[:], in_=tab_s[:].indirect(idx[:]))
        rounded_g0 = tenant(ROUNDED_G0, [P, 2, KP * PACK], BF16, "rounded_g0")
        round_w1(0, 0, rounded_g0[:, 0, :], range(PACK), on_vector=False)
        round_w1(1, 0, rounded_g0[:, 1, :], range(0, 2), on_vector=True)
        round_w1(1, 0, rounded_g0[:, 1, :], range(2, PACK), on_vector=False)
        for a in range(2):
            quantize_w1(a, 0, rounded_g0[:, a, :])
        v_w.append(tenant(ROUNDED_G0, [P, S], U32, "v_w1"))
        for half in range(2):
            gather_words(1, half * BANK, (half + 1) * BANK)

        load_wg(2)
        load_wg(3)
        w1_raw[(0, 1)] = load_w1(0, 1)

        h_first = keep.tile([P, S], F32, name="h_first", align_bytes=64)
        nc.vector.scalar_tensor_tensor(
            out=h_first[:, 0:BANK],
            in0=first_product(0, 0, 0)[:],
            scalar=bias[:, 0, 0:1],
            in1=wg[0][:, 0:BANK],
            op0=ADD,
            op1=MULT,
        )
        place(h_first, 0, 0, BANK)
        add_bias(h_first, 0, 0, 1)
        weigh(h_first, 0, BANK, S)
        place(h_first, 0, BANK, S)
        hs = {(0, t): signals(0, t) for t in range(1, PACK)}
        for t in range(1, PACK):
            weigh(hs[(0, t)], t)

        rounded_g1 = [
            tenant(buffer, [P, KP * PACK], BF16, "rounded_g1")
            for buffer in (ROUNDED_A0G1, ROUNDED_A1G1)
        ]
        for a in (1, 0):
            round_w1(a, 1, rounded_g1[a][:], range(PACK), on_vector=False)
        old_rows = [load_old_rows(t) for t in range(PACK)]
        nc.sync.dma_start(
            out=w4_w[:].bitcast(I32), in_=w4_words.rearrange("a p e -> p a e").bitcast(I32)
        )
        for q in range(P // QP):
            nc.sync.dma_start(
                out=w4_s[QP * q : QP * q + QROWS, :].rearrange("r (a n) -> r a n", a=2).bitcast(I32),
                in_=w4_scales[:, QROWS * q : QROWS * (q + 1), :]
                .rearrange("a r n -> r a n")
                .bitcast(I32),
            )

        place(hs[(0, 1)], 1)
        gate = gate_rows(0)
        w1_w.append(tenant(H_A, [P, 2 * KP], U32, "w1_w1"))
        for a in (1, 0):
            quantize_w1(a, 1, rounded_g1[a][:])

        z_rows = tenant(ROUNDED_A1G1, [P, PACK, T2], BF16, "z_rows")
        nc.gpsimd.tensor_tensor(z_rows[:, 0, :], old_rows[0][:], gate[:], MULT)
        place(hs[(0, 2)], 2)
        hs[(1, 0)] = signals(1, 0)
        weigh(hs[(1, 0)], 0)
        next_to_place = {1: (0, 3), 2: (1, 0)}
        for t in range(1, PACK):
            gate = gate_rows(t)
            hs[(1, t)] = signals(1, t)
            weigh(hs[(1, t)], t)
            nc.gpsimd.tensor_tensor(z_rows[:, t, :], old_rows[t][:], gate[:], MULT)
            if t in next_to_place:
                place(hs[next_to_place[t]], next_to_place[t][1])

        old_chunks = [load_old_chunk(c) for c in range(CHUNKS)]
        gates = [
            tenant(GATE_CHUNK_BUFFER[c], [P, PACK, BANK], F32, "gate_chunk") for c in range(CHUNKS)
        ]
        for t in range(2):
            place(hs[(1, t + 1)], t + 1)
            gate_chunks(t)

        z_left = tenant(ROUNDED_G0, [P, 2 * BANK * PACK], BF16, "z_left")
        nc.gpsimd.tensor_scalar(
            z_left[:].rearrange("p (c t) -> p c t", t=PACK),
            z_rows[:, :, 0 : 2 * BANK].rearrange("p t c -> p c t"),
            1.0,
            0.0,
            MULT,
            ADD,
        )
        z_right = tenant(H_B, [P, 2 * BANK * PACK], BF16, "z_right")
        right_part = {
            c: z_right[:, (c - 2) * BANK * PACK : (c - 1) * BANK * PACK] for c in range(2, CHUNKS)
        }
        for c in range(2, CHUNKS):
            interleave_on_scalar(right_part[c], z_rows[:, :, c * BANK : (c + 1) * BANK])

        early_rows = tenant(H_A, [P, PACK, BANK], BF16, "early_rows")
        nc.gpsimd.tensor_tensor(
            early_rows[:, 0:2, :], old_chunks[0][:, 0:2, :], gates[0][:, 0:2, :], MULT
        )
        place(hs[(1, 3)], 3)
        gate_chunks(2)
        nc.gpsimd.tensor_tensor(early_rows[:, 2, :], old_chunks[0][:, 2, :], gates[0][:, 2, :], MULT)
        gate_chunks(3)

        accs = {}
        left_codes = tenant(H_D, [P, 2 * BANK], U32, "z_w0")
        quantize_z(0, 0, 2 * BANK, left_codes[:], z_left[:])
        for c in (1, 0):
            z_w[(0, c)] = left_codes[:, c * BANK : (c + 1) * BANK]
            open_chunk(c)

        nc.vector.tensor_tensor(early_rows[:, 3, :], old_chunks[0][:, 3, :], gates[0][:, 3, :], MULT)
        z_early = tenant(Z_CHUNK_BUFFER[0], [P, BANK * PACK], BF16, "z_early")
        interleave_on_scalar(z_early[:], early_rows[:])

        def commands(c):
            z_bf = tenant(Z_CHUNK_BUFFER[c], [P, BANK * PACK], BF16, "z_bf")
            nc.vector.tensor_tensor(
                z_bf[:].rearrange("p (c i t) -> p c t i", i=2, t=PACK),
                old_chunks[c][:].rearrange("p t (c i) -> p c t i", i=2),
                gates[c][:].rearrange("p t (c i) -> p c t i", i=2),
                MULT,
            )
            return z_bf

        def quantize_right(c):
            z_w[(0, c)] = tenant(RIGHT_CODES_BUFFER[c], [P, BANK], U32, "z_w0")[:]
            quantize_z(0, c * BANK, (c + 1) * BANK, z_w[(0, c)], right_part[c])

        def respond(c, z_bf):
            quantize_z(1, c * BANK, (c + 1) * BANK, z_w[(1, c)], z_bf[:])
            finish_chunk(c)

        z_bf = commands(1)
        quantize_right(2)
        respond(1, z_bf)
        respond(0, z_early)
        open_chunk(2)
        z_bf = commands(2)
        quantize_right(3)
        open_chunk(3)
        respond(2, z_bf)
        respond(3, commands(3))
